import numpy as np
import ml_dtypes


def mxq(x, axis, fmt="e4m3"):
    dtype, down = {"e4m3": (ml_dtypes.float8_e4m3fn, 7), "e5m2": (ml_dtypes.float8_e5m2, 14)}[fmt]
    v = np.moveaxis(np.asarray(x, np.float32).astype(ml_dtypes.bfloat16).astype(np.float64), axis, -1)
    blocks = v.reshape(v.shape[:-1] + (-1, 32))
    amax = np.abs(blocks).max(-1, keepdims=True)
    byte = np.maximum(np.where(amax > 0, np.frexp(amax)[1] - 1 + 127, 0) - down, 1)
    scale = np.exp2(byte - 127.0)
    codes = (blocks / scale).astype(np.float32).astype(dtype).astype(np.float64)
    return np.moveaxis((codes * scale).reshape(v.shape), -1, axis)


WIDE = False


def mx_kscale(k):
    if not WIDE:
        return np.ones(k)
    levels = np.array([10, -10, 5, -5, 0])
    if k % 512:
        return np.exp2(np.random.permutation(np.resize(levels, k // 32))).repeat(32)
    a = np.empty((k // 512, 16))
    for p in range(k // 512):
        a[p, :8] = np.random.permutation(np.resize(levels, 8))
        for g in range(8):
            far = levels[np.abs(levels - a[p, g]) >= 10]
            a[p, g + 8] = far[np.random.randint(len(far))]
    return np.exp2(a.ravel()).repeat(32)


def f64(x):
    return np.asarray(x).astype(np.float64)


def striped(idx):
    return np.tile(idx.reshape(-1, 16).T, (8, 1)).astype(np.uint16)


def unstriped(offs):
    return offs[:16].T.reshape(-1).astype(np.int64)


K, T, D, S, V, N = 512, 512, 6, 1536, 256, 512


def setup_inputs():
    n = np.random.standard_normal
    s = mx_kscale(K)[:, None]
    return {
        "xT": (n((K, T)) * s).astype(np.float32),
        "w": (n((K, N)) / np.sqrt(K) / s).astype(np.float32),
        "b": (0.3 * n((N, 1))).astype(np.float32),
        "gate": np.tile(np.random.uniform(0.2, 1.0, (D, 1, V)) / np.sqrt(D), (1, N, 1)).astype(np.float32),
        "pos1": striped(np.random.permutation(T)[:V]),
        "pos2": striped(np.random.permutation(T)[:V]),
        "pos3": striped(np.random.permutation(T)[:V]),
        "pos4": striped(np.random.permutation(T)[:V]),
        "pos5": striped(np.random.permutation(T)[:V]),
        "pos6": striped(np.random.permutation(T)[:V]),
    }


def reference(xT, w, b, gate, pos1, pos2, pos3, pos4, pos5, pos6):
    y = mxq(f64(w), 0, "e4m3").T @ mxq(f64(xT), 0, "e4m3")
    y = y + f64(b)
    return sum(f64(gate[d]) * y[:, unstriped(p)] for d, p in enumerate((pos1, pos2, pos3, pos4, pos5, pos6)))

@@ -1,0 +1,174 @@
+from contextlib import ExitStack
+
+import concourse.mybir as mybir
+from concourse.masks import make_identity
+
+K, T, D, V, N = 512, 512, 6, 256, 512
+P = 128
+PACK = 4
+BLOCKS = N // P
+HALF = T // 2
+FLOPS = 2 * K * N * T + 2 * D * N * V
+BYTES = 4 * (K * T + K * N + N + D * V + N * V) + D * P * (V // 16) * 2
+
+F32 = mybir.dt.float32
+BF16 = mybir.dt.bfloat16
+U32 = mybir.dt.uint32
+U16 = mybir.dt.uint16
+U8 = mybir.dt.uint8
+FP8X4 = mybir.dt.float8_e4m3fn_x4
+MULT = mybir.AluOpType.mult
+ADD = mybir.AluOpType.add
+IDENTITY = mybir.ActivationFunctionType.Identity
+
+VECTOR_COLS = 176
+PE_TURNS_LAST = 4
+
+
+def tile_picked_agg_lin_bias_sub_l_kernel(
+    tc, xT, w, b, gate, pos1, pos2, pos3, pos4, pos5, pos6, out
+):
+    nc = tc.nc
+    lists_hbm = (pos1, pos2, pos3, pos4, pos5, pos6)
+    x_rows = xT.rearrange("(p j) t -> p j t", j=PACK)
+    w_rows = w.rearrange("(p j) m -> p j m", j=PACK)
+
+    with ExitStack() as ctx:
+        keep = ctx.enter_context(tc.tile_pool(name="keep", bufs=1))
+        psum = ctx.enter_context(tc.psum_pool(name="psum", bufs=1))
+
+        def load(name, shape, dtype, src):
+            tile = keep.tile(shape, dtype, name=name, align_bytes=64)
+            nc.sync.dma_start(tile[:], src)
+            return tile
+
+        def load_list(d):
+            return load("list%d" % d, [P, V // 16], U16, lists_hbm[d])
+
+        def load_gates(d0, d1):
+            tile = load("gates%d" % d0, [P, d1 - d0, V], F32, gate[d0:d1, 0:P, :].rearrange("d p v -> p d v"))
+            return [tile[:, i, :] for i in range(d1 - d0)]
+
+        w_first = load("w_first", [P, PACK, P], F32, w_rows[:, :, 0:P])
+        x_raw = [load("x_raw%d" % h, [P, PACK, HALF], F32, x_rows[:, :, h * HALF : (h + 1) * HALF]) for h in range(2)]
+        bias_first = load("bias_first", [P, 1], F32, b[0:P, :])
+        lists = [load_list(0)]
+        gates = load_gates(0, 1)
+        lists.append(load_list(1))
+        gates.extend(load_gates(1, 3))
+        w_second = load("w_second", [P, PACK, P], F32, w_rows[:, :, P : 2 * P])
+        lists.append(load_list(2))
+        lists.append(load_list(3))
+        gates.extend(load_gates(3, 6))
+        lists.append(load_list(4))
+        lists.append(load_list(5))
+        with nc.allow_non_contiguous_dma(reason="one bias value to a partition"):
+            bias_rest = load("bias_rest", [P, BLOCKS - 1, 1], F32, b[P:N, :].rearrange("(c p) o -> p c o", p=P))
+        w_rest = load("w_rest", [P, PACK, 2 * P], F32, w_rows[:, :, 2 * P : N])
+        w_raw = [w_first[:], w_second[:], w_rest[:, :, 0:P], w_rest[:, :, P : 2 * P]]
+        bias = [bias_first[:]] + [bias_rest[:, c, :] for c in range(BLOCKS - 1)]
+
+        warm = keep.tile([P, 2], F32, name="warm")
+        nc.gpsimd.memset(warm[:, 0:1], 0.0)
+        nc.scalar.activation(warm[:, 1:2], warm[:, 0:1], IDENTITY, bias=warm[:, 0:1])
+        ident = keep.tile([P, P], F32, name="ident")
+        make_identity(nc, ident[:])
+
+        def interleave(copy, grouped, raw):
+            copy(
+                grouped.rearrange("p (c i) j -> p c j i", i=4),
+                raw.rearrange("p j (c i) -> p c j i", i=4),
+            )
+
+        def quantise(codes, scales, grouped):
+            nc.vector.quantize_mx(
+                out=codes.bitcast(FP8X4), scales=scales, in_=grouped.rearrange("p c j -> p (c j)")
+            )
+
+        w_codes, w_scales = [], []
+
+        def prepare_w(blk, copy):
+            grouped = keep.tile([P, P, PACK], BF16, name="w_grouped%d" % blk, align_bytes=64)
+            codes = keep.tile([P, P], U32, name="w_codes%d" % blk, align_bytes=64)
+            scales = keep.tile([P, P], U8, name="w_scales%d" % blk, align_bytes=64)
+            interleave(copy, grouped[:], w_raw[blk])
+            quantise(codes[:], scales[:], grouped[:])
+            w_codes.append(codes)
+            w_scales.append(scales)
+
+        x_codes = keep.tile([P, T], U32, name="x_codes", align_bytes=64)
+        x_scales = keep.tile([P, T], U8, name="x_scales", align_bytes=64)
+
+        def project(blk, acc, cols):
+            nc.tensor.matmul_mx(
+                out=acc,
+                lhsT=w_codes[blk][:].bitcast(FP8X4),
+                lhsT_scale=w_scales[blk][:],
+                rhs=x_codes[:, cols].bitcast(FP8X4),
+                rhs_scale=x_scales[:, cols],
+                start=True,
+                stop=True,
+            )
+
+        y = [keep.tile([P, T], F32, name="y%d" % blk) for blk in range(BLOCKS)]
+
+        prepare_w(0, nc.vector.tensor_copy)
+        halves = [slice(0, HALF), slice(HALF, T)]
+        x_grouped = [keep.tile([P, HALF, PACK], BF16, name="x_grouped%d" % h, align_bytes=64) for h in range(2)]
+        acc_half = [psum.tile([P, HALF], F32, name="acc_half%d" % h) for h in range(2)]
+        interleave(nc.vector.tensor_copy, x_grouped[0][:], x_raw[0][:])
+        quantise(x_codes[:, halves[0]], x_scales[:, halves[0]], x_grouped[0][:])
+        project(0, acc_half[0][:], halves[0])
+        interleave(nc.vector.tensor_copy, x_grouped[1][:, 0:VECTOR_COLS, :], x_raw[1][:, :, 0:VECTOR_COLS])
+        interleave(nc.scalar.copy, x_grouped[1][:, VECTOR_COLS:HALF, :], x_raw[1][:, :, VECTOR_COLS:HALF])
+        quantise(x_codes[:, halves[1]], x_scales[:, halves[1]], x_grouped[1][:])
+        project(0, acc_half[1][:], halves[1])
+        nc.vector.tensor_scalar(y[0][:, halves[0]], acc_half[0][:], bias[0], None, ADD)
+        nc.scalar.activation(y[0][:, halves[1]], acc_half[1][:], IDENTITY, bias=bias[0])
+
+        for blk in range(BLOCKS):
+            last = blk == BLOCKS - 1
+            pe_turns = PE_TURNS_LAST if last else D
+            sum_t = psum.tile([P, 2, P], F32, name="sum_t", bufs=2)
+            for d in range(pe_turns):
+                product = keep.tile([P, V], F32, name="product%d_%d" % (blk, d))
+                nc.vector.tensor_tensor(product[:], y[blk][:].indirect(lists[d][:]), gates[d], MULT)
+                for h in range(2):
+                    nc.tensor.matmul(
+                        sum_t[:, h, :],
+                        product[:, h * P : (h + 1) * P],
+                        ident[:],
+                        start=(d == 0 and h == 0),
+                        stop=(d == pe_turns - 1 and h == 1),
+                        is_transpose=True,
+                    )
+                if d == 1 and not last:
+                    prepare_w(blk + 1, nc.scalar.copy)
+                    acc = psum.tile([P, T], F32, name="acc", bufs=2)
+                    project(blk + 1, acc[:], slice(0, T))
+                    nc.scalar.activation(y[blk + 1][:], acc[:], IDENTITY, bias=bias[blk + 1])
+
+            sum_t_sb = keep.tile([P, 2, P], F32, name="sum_t_sb%d" % blk)
+            nc.scalar.copy(sum_t_sb[:], sum_t[:])
+            total = psum.tile([P, 2, P], F32, name="total", bufs=2)
+            for h in range(2):
+                nc.tensor.transpose(total[:, h, :], sum_t_sb[:, h, :], ident[:])
+            result = keep.tile([P, 2, P], F32, name="result%d" % blk)
+            out_rows = out[blk * P : (blk + 1) * P, :]
+            if not last:
+                nc.scalar.copy(result[:], total[:])
+                nc.sync.dma_start(out_rows, result[:].rearrange("p h v -> p (h v)"))
+            else:
+                fifth = keep.tile([P, V], F32, name="fifth")
+                nc.vector.tensor_tensor(fifth[:], y[blk][:].indirect(lists[4][:]), gates[4], MULT)
+                sixth = [keep.tile([P, P], F32, name="sixth%d" % h) for h in range(2)]
+                pair = [keep.tile([P, P], F32, name="pair%d" % h) for h in range(2)]
+                for h in range(2):
+                    nc.vector.tensor_tensor(
+                        sixth[h][:], y[blk][:].indirect(lists[5][:, h * 8 : (h + 1) * 8]), gates[5][:, h * P : (h + 1) * P], MULT
+                    )
+                for h in range(2):
+                    nc.vector.tensor_tensor(pair[h][:], fifth[:, h * P : (h + 1) * P], sixth[h][:], ADD)
+                for h in range(2):
+                    nc.vector.tensor_tensor(result[:, h, :], total[:, h, :], pair[h][:], ADD)
+                nc.sync.dma_start(out_rows, result[:].rearrange("p h v -> p (h v)"))

@@ -1,7 +1,6 @@
 from contextlib import ExitStack
 
 import concourse.mybir as mybir
-from concourse.masks import make_identity
 
 K, T, D, V, N = 512, 512, 6, 256, 512
 P = 128
@@ -21,7 +20,10 @@ MULT = mybir.AluOpType.mult
 ADD = mybir.AluOpType.add
 IDENTITY = mybir.ActivationFunctionType.Identity
 
-VECTOR_COLS = 176
+GATE_ROWS = 8
+GATE_STEP = D * N // GATE_ROWS
+GATE_AT = P - GATE_ROWS
+BIAS_AT = GATE_AT - BLOCKS
 PE_TURNS_LAST = 4
 
 
@@ -42,37 +44,58 @@ def tile_picked_agg_lin_bias_sub_l_kernel(
             nc.sync.dma_start(tile[:], src)
             return tile
 
-        def load_list(d):
-            return load("list%d" % d, [P, V // 16], U16, lists_hbm[d])
-
-        def load_gates(d0, d1):
-            tile = load("gates%d" % d0, [P, d1 - d0, V], F32, gate[d0:d1, 0:P, :].rearrange("d p v -> p d v"))
-            return [tile[:, i, :] for i in range(d1 - d0)]
+        rows = keep.tile([P, V], F32, name="rows")
+        gate_rows = gate.rearrange("d m v -> (d m) v").rearrange("(r s) v -> r s v", r=GATE_ROWS)
+        nc.sync.dma_start(rows[GATE_AT:P, :], gate_rows[:, 0, :])
+        nc.sync.dma_start(rows[BIAS_AT:GATE_AT, 0:P], b.rearrange("(c p) o -> c (p o)", p=P))
 
         w_first = load("w_first", [P, PACK, P], F32, w_rows[:, :, 0:P])
         x_raw = [load("x_raw%d" % h, [P, PACK, HALF], F32, x_rows[:, :, h * HALF : (h + 1) * HALF]) for h in range(2)]
-        bias_first = load("bias_first", [P, 1], F32, b[0:P, :])
-        lists = [load_list(0)]
-        gates = load_gates(0, 1)
-        lists.append(load_list(1))
-        gates.extend(load_gates(1, 3))
+        lists = [load("list0", [P, V // 16], U16, lists_hbm[0])]
         w_second = load("w_second", [P, PACK, P], F32, w_rows[:, :, P : 2 * P])
-        lists.append(load_list(2))
-        lists.append(load_list(3))
-        gates.extend(load_gates(3, 6))
-        lists.append(load_list(4))
-        lists.append(load_list(5))
-        with nc.allow_non_contiguous_dma(reason="one bias value to a partition"):
-            bias_rest = load("bias_rest", [P, BLOCKS - 1, 1], F32, b[P:N, :].rearrange("(c p) o -> p c o", p=P))
+        lists.append(load("list1", [P, V // 16], U16, lists_hbm[1]))
         w_rest = load("w_rest", [P, PACK, 2 * P], F32, w_rows[:, :, 2 * P : N])
-        w_raw = [w_first[:], w_second[:], w_rest[:, :, 0:P], w_rest[:, :, P : 2 * P]]
-        bias = [bias_first[:]] + [bias_rest[:, c, :] for c in range(BLOCKS - 1)]
+        lists.extend([load("list%d" % d, [P, V // 16], U16, lists_hbm[d]) for d in range(2, D)])
 
-        warm = keep.tile([P, 2], F32, name="warm")
-        nc.gpsimd.memset(warm[:, 0:1], 0.0)
-        nc.scalar.activation(warm[:, 1:2], warm[:, 0:1], IDENTITY, bias=warm[:, 0:1])
+        ones = keep.tile([P, P], F32, name="ones")
+        nc.vector.memset(ones[:], 1.0)
+        warm = keep.tile([P, 1], F32, name="warm")
+        nc.scalar.activation(warm[:], ones[:, 0:1], IDENTITY, bias=ones[:, 0:1])
+        quadrant = keep.tile([P, 1], F32, name="quadrant")
+        nc.vector.memset(quadrant[0:32, :], 0.0)
+        count = keep.tile([P, P], F32, name="count", align_bytes=64)
+        nc.vector.tensor_tensor_scan(count[:], ones[:], ones[:], 0.0, MULT, ADD)
+        for q in range(1, 4):
+            nc.vector.memset(quadrant[32 * q : 32 * (q + 1), :], 32.0 * q)
+        within = keep.tile([P, 32], F32, name="within", align_bytes=64)
+        nc.vector.transpose(within[:], count[:, 0:32])
+        nc.vector.memset(rows[0:BIAS_AT, :], 0.0)
+        nc.vector.memset(rows[96:GATE_AT, P:V], 0.0)
         ident = keep.tile([P, P], F32, name="ident")
-        make_identity(nc, ident[:])
+        nc.vector.tensor_scalar(
+            ident[:], count[:], within[:, 0:1], quadrant[:], mybir.AluOpType.subtract, mybir.AluOpType.is_equal
+        )
+
+        turned = psum.tile([P, 2, P], F32, name="turned", tag="total", bufs=2)
+        for h in range(2):
+            nc.tensor.transpose(turned[:, h, :], rows[:, h * P : (h + 1) * P], ident[:])
+        columns = keep.tile([P, 2, 16], F32, name="columns")
+        nc.scalar.copy(columns[:], turned[:, :, P - 16 : P])
+        bias = [columns[:, 0, 4 + blk : 5 + blk] for blk in range(BLOCKS)]
+        gates = []
+
+        def spread_gates(pair, tag):
+            spread = psum.tile([P, 2, 2, P], F32, name="spread", tag=tag)
+            for i in range(2):
+                r = 8 - (-(2 * pair + i) * N // GATE_STEP)
+                for h in range(2):
+                    nc.tensor.transpose(spread[:, i, h, :], columns[:, h, r : r + 1].to_broadcast([P, P]), ident[:])
+            gate_pair = keep.tile([P, 2, V], F32, name="gate_pair%d" % pair)
+            nc.scalar.copy(gate_pair[:], spread[:].rearrange("p i h v -> p i (h v)"))
+            gates.extend([gate_pair[:, 0, :], gate_pair[:, 1, :]])
+
+        spread_gates(0, "sum0")
+        spread_gates(1, "sum1")
 
         def interleave(copy, grouped, raw):
             copy(
@@ -87,14 +110,16 @@ def tile_picked_agg_lin_bias_sub_l_kernel(
 
         w_codes, w_scales = [], []
 
-        def prepare_w(blk, copy):
-            grouped = keep.tile([P, P, PACK], BF16, name="w_grouped%d" % blk, align_bytes=64)
-            codes = keep.tile([P, P], U32, name="w_codes%d" % blk, align_bytes=64)
-            scales = keep.tile([P, P], U8, name="w_scales%d" % blk, align_bytes=64)
-            interleave(copy, grouped[:], w_raw[blk])
+        def prepare_w(name, raw, copy, tag):
+            width = raw.shape[2]
+            grouped = keep.tile([P, width, PACK], BF16, name="grouped_" + name, tag=tag, align_bytes=64)
+            codes = keep.tile([P, width], U32, name="codes_" + name, align_bytes=64)
+            scales = keep.tile([P, width], U8, name="scales_" + name, align_bytes=64)
+            interleave(copy, grouped[:], raw[:])
             quantise(codes[:], scales[:], grouped[:])
-            w_codes.append(codes)
-            w_scales.append(scales)
+            for c0 in range(0, width, P):
+                w_codes.append(codes[:, c0 : c0 + P])
+                w_scales.append(scales[:, c0 : c0 + P])
 
         x_codes = keep.tile([P, T], U32, name="x_codes", align_bytes=64)
         x_scales = keep.tile([P, T], U8, name="x_scales", align_bytes=64)
@@ -102,8 +127,8 @@ def tile_picked_agg_lin_bias_sub_l_kernel(
         def project(blk, acc, cols):
             nc.tensor.matmul_mx(
                 out=acc,
-                lhsT=w_codes[blk][:].bitcast(FP8X4),
-                lhsT_scale=w_scales[blk][:],
+                lhsT=w_codes[blk].bitcast(FP8X4),
+                lhsT_scale=w_scales[blk],
                 rhs=x_codes[:, cols].bitcast(FP8X4),
                 rhs_scale=x_scales[:, cols],
                 start=True,
@@ -112,26 +137,35 @@ def tile_picked_agg_lin_bias_sub_l_kernel(
 
         y = [keep.tile([P, T], F32, name="y%d" % blk) for blk in range(BLOCKS)]
 
-        prepare_w(0, nc.vector.tensor_copy)
-        halves = [slice(0, HALF), slice(HALF, T)]
+        def project_block(blk):
+            acc = psum.tile([P, T], F32, name="acc", tag="acc0" if blk == 1 else "acc%d" % blk)
+            project(blk, acc[:], slice(0, T))
+            nc.scalar.activation(y[blk][:], acc[:], IDENTITY, bias=bias[blk])
+
+        prepare_w("first", w_first, nc.vector.tensor_copy, "grouped_first")
         x_grouped = [keep.tile([P, HALF, PACK], BF16, name="x_grouped%d" % h, align_bytes=64) for h in range(2)]
-        acc_half = [psum.tile([P, HALF], F32, name="acc_half%d" % h) for h in range(2)]
         interleave(nc.vector.tensor_copy, x_grouped[0][:], x_raw[0][:])
-        quantise(x_codes[:, halves[0]], x_scales[:, halves[0]], x_grouped[0][:])
-        project(0, acc_half[0][:], halves[0])
-        interleave(nc.vector.tensor_copy, x_grouped[1][:, 0:VECTOR_COLS, :], x_raw[1][:, :, 0:VECTOR_COLS])
-        interleave(nc.scalar.copy, x_grouped[1][:, VECTOR_COLS:HALF, :], x_raw[1][:, :, VECTOR_COLS:HALF])
-        quantise(x_codes[:, halves[1]], x_scales[:, halves[1]], x_grouped[1][:])
-        project(0, acc_half[1][:], halves[1])
-        nc.vector.tensor_scalar(y[0][:, halves[0]], acc_half[0][:], bias[0], None, ADD)
-        nc.scalar.activation(y[0][:, halves[1]], acc_half[1][:], IDENTITY, bias=bias[0])
+        quantise(x_codes[:, 0:HALF], x_scales[:, 0:HALF], x_grouped[0][:])
+        for c0 in (0, P):
+            interleave(nc.vector.tensor_copy, x_grouped[1][:, c0 : c0 + P, :], x_raw[1][:, :, c0 : c0 + P])
+        for c0 in (0, P):
+            cols = slice(HALF + c0, HALF + c0 + P)
+            quantise(x_codes[:, cols], x_scales[:, cols], x_grouped[1][:, c0 : c0 + P, :])
+        for piece, (c0, c1) in enumerate(((0, HALF), (HALF, HALF + P), (HALF + P, T))):
+            acc = psum.tile([P, c1 - c0], F32, name="acc", tag="acc%d" % piece)
+            project(0, acc[:], slice(c0, c1))
+            nc.scalar.activation(y[0][:, c0:c1], acc[:], IDENTITY, bias=bias[0])
+        spread_gates(2, "acc1")
+        prepare_w("second", w_second, nc.vector.tensor_copy, "grouped_second")
+        project_block(1)
 
         for blk in range(BLOCKS):
             last = blk == BLOCKS - 1
             pe_turns = PE_TURNS_LAST if last else D
-            sum_t = psum.tile([P, 2, P], F32, name="sum_t", bufs=2)
+            sum_t = psum.tile([P, 2, P], F32, name="sum_t", tag="sum%d" % (blk % 2))
             for d in range(pe_turns):
-                product = keep.tile([P, V], F32, name="product%d_%d" % (blk, d))
+                slot = "slot%d" % ((D * blk + d) % 4)
+                product = keep.tile([P, V], F32, name="product%d_%d" % (blk, d), tag=slot)
                 nc.vector.tensor_tensor(product[:], y[blk][:].indirect(lists[d][:]), gates[d], MULT)
                 for h in range(2):
                     nc.tensor.matmul(
@@ -142,11 +176,10 @@ def tile_picked_agg_lin_bias_sub_l_kernel(
                         stop=(d == pe_turns - 1 and h == 1),
                         is_transpose=True,
                     )
-                if d == 1 and not last:
-                    prepare_w(blk + 1, nc.scalar.copy)
-                    acc = psum.tile([P, T], F32, name="acc", bufs=2)
-                    project(blk + 1, acc[:], slice(0, T))
-                    nc.scalar.activation(y[blk + 1][:], acc[:], IDENTITY, bias=bias[blk + 1])
+                if blk == 0 and d == 3:
+                    prepare_w("rest", w_rest, nc.scalar.copy, "codes_second")
+                    project_block(2)
+                    project_block(3)
 
             sum_t_sb = keep.tile([P, 2, P], F32, name="sum_t_sb%d" % blk)
             nc.scalar.copy(sum_t_sb[:], sum_t[:])
@@ -159,16 +192,16 @@ def tile_picked_agg_lin_bias_sub_l_kernel(
                 nc.scalar.copy(result[:], total[:])
                 nc.sync.dma_start(out_rows, result[:].rearrange("p h v -> p (h v)"))
             else:
-                fifth = keep.tile([P, V], F32, name="fifth")
+                fifth = keep.tile([P, V], F32, name="fifth", tag="slot2")
                 nc.vector.tensor_tensor(fifth[:], y[blk][:].indirect(lists[4][:]), gates[4], MULT)
-                sixth = [keep.tile([P, P], F32, name="sixth%d" % h) for h in range(2)]
+                sixth = keep.tile([P, V], F32, name="sixth", tag="slot3")
                 pair = [keep.tile([P, P], F32, name="pair%d" % h) for h in range(2)]
                 for h in range(2):
                     nc.vector.tensor_tensor(
-                        sixth[h][:], y[blk][:].indirect(lists[5][:, h * 8 : (h + 1) * 8]), gates[5][:, h * P : (h + 1) * P], MULT
+                        sixth[:, h * P : (h + 1) * P], y[blk][:].indirect(lists[5][:, h * 8 : (h + 1) * 8]), gates[5][:, h * P : (h + 1) * P], MULT
                     )
                 for h in range(2):
-                    nc.vector.tensor_tensor(pair[h][:], fifth[:, h * P : (h + 1) * P], sixth[h][:], ADD)
+                    nc.vector.tensor_tensor(pair[h][:], fifth[:, h * P : (h + 1) * P], sixth[:, h * P : (h + 1) * P], ADD)
                 for h in range(2):
                     nc.vector.tensor_tensor(result[:, h, :], total[:, h, :], pair[h][:], ADD)
                 nc.sync.dma_start(out_rows, result[:].rearrange("p h v -> p (h v)"))

@@ -53,9 +53,9 @@ def tile_picked_agg_lin_bias_sub_l_kernel(
         x_raw = [load("x_raw%d" % h, [P, PACK, HALF], F32, x_rows[:, :, h * HALF : (h + 1) * HALF]) for h in range(2)]
         lists = [load("list0", [P, V // 16], U16, lists_hbm[0])]
         w_second = load("w_second", [P, PACK, P], F32, w_rows[:, :, P : 2 * P])
-        lists.append(load("list1", [P, V // 16], U16, lists_hbm[1]))
+        lists.extend([load("list%d" % d, [P, V // 16], U16, lists_hbm[d]) for d in range(1, 4)])
         w_rest = load("w_rest", [P, PACK, 2 * P], F32, w_rows[:, :, 2 * P : N])
-        lists.extend([load("list%d" % d, [P, V // 16], U16, lists_hbm[d]) for d in range(2, D)])
+        lists.extend([load("list%d" % d, [P, V // 16], U16, lists_hbm[d]) for d in range(4, D)])
 
         ones = keep.tile([P, P], F32, name="ones")
         nc.vector.memset(ones[:], 1.0)
@@ -115,7 +115,7 @@ def tile_picked_agg_lin_bias_sub_l_kernel(
             grouped = keep.tile([P, width, PACK], BF16, name="grouped_" + name, tag=tag, align_bytes=64)
             codes = keep.tile([P, width], U32, name="codes_" + name, align_bytes=64)
             scales = keep.tile([P, width], U8, name="scales_" + name, align_bytes=64)
-            interleave(copy, grouped[:], raw[:])
+            interleave(copy, grouped[:], raw)
             quantise(codes[:], scales[:], grouped[:])
             for c0 in range(0, width, P):
                 w_codes.append(codes[:, c0 : c0 + P])
@@ -142,7 +142,7 @@ def tile_picked_agg_lin_bias_sub_l_kernel(
             project(blk, acc[:], slice(0, T))
             nc.scalar.activation(y[blk][:], acc[:], IDENTITY, bias=bias[blk])
 
-        prepare_w("first", w_first, nc.vector.tensor_copy, "grouped_first")
+        prepare_w("first", w_first[:], nc.vector.tensor_copy, "grouped_first")
         x_grouped = [keep.tile([P, HALF, PACK], BF16, name="x_grouped%d" % h, align_bytes=64) for h in range(2)]
         interleave(nc.vector.tensor_copy, x_grouped[0][:], x_raw[0][:])
         quantise(x_codes[:, 0:HALF], x_scales[:, 0:HALF], x_grouped[0][:])
@@ -156,7 +156,7 @@ def tile_picked_agg_lin_bias_sub_l_kernel(
             project(0, acc[:], slice(c0, c1))
             nc.scalar.activation(y[0][:, c0:c1], acc[:], IDENTITY, bias=bias[0])
         spread_gates(2, "acc1")
-        prepare_w("second", w_second, nc.vector.tensor_copy, "grouped_second")
+        prepare_w("second", w_second[:], nc.vector.tensor_copy, "grouped_second")
         project_block(1)
 
         for blk in range(BLOCKS):
@@ -176,9 +176,11 @@ def tile_picked_agg_lin_bias_sub_l_kernel(
                         stop=(d == pe_turns - 1 and h == 1),
                         is_transpose=True,
                     )
-                if blk == 0 and d == 3:
-                    prepare_w("rest", w_rest, nc.scalar.copy, "codes_second")
+                if blk == 0 and d == 4:
+                    prepare_w("third", w_rest[:, :, 0:P], nc.scalar.copy, "codes_second")
                     project_block(2)
+                if blk == 0 and d == 5:
+                    prepare_w("fourth", w_rest[:, :, P : 2 * P], nc.scalar.copy, "scales_second")
                     project_block(3)
 
             sum_t_sb = keep.tile([P, 2, P], F32, name="sum_t_sb%d" % blk)

from contextlib import ExitStack

import concourse.mybir as mybir

K, T, D, V, N = 512, 512, 6, 256, 512
P = 128
PACK = 4
BLOCKS = N // P
HALF = T // 2
FLOPS = 2 * K * N * T + 2 * D * N * V
BYTES = 4 * (K * T + K * N + N + D * V + N * V) + D * P * (V // 16) * 2

F32 = mybir.dt.float32
BF16 = mybir.dt.bfloat16
U32 = mybir.dt.uint32
U16 = mybir.dt.uint16
U8 = mybir.dt.uint8
FP8X4 = mybir.dt.float8_e4m3fn_x4
MULT = mybir.AluOpType.mult
ADD = mybir.AluOpType.add
IDENTITY = mybir.ActivationFunctionType.Identity

GATE_ROWS = 8
GATE_STEP = D * N // GATE_ROWS
GATE_AT = P - GATE_ROWS
BIAS_AT = GATE_AT - BLOCKS
PE_TURNS_LAST = 4


def tile_picked_agg_lin_bias_sub_l_kernel(
    tc, xT, w, b, gate, pos1, pos2, pos3, pos4, pos5, pos6, out
):
    nc = tc.nc
    lists_hbm = (pos1, pos2, pos3, pos4, pos5, pos6)
    x_rows = xT.rearrange("(p j) t -> p j t", j=PACK)
    w_rows = w.rearrange("(p j) m -> p j m", j=PACK)

    with ExitStack() as ctx:
        keep = ctx.enter_context(tc.tile_pool(name="keep", bufs=1))
        psum = ctx.enter_context(tc.psum_pool(name="psum", bufs=1))

        def load(name, shape, dtype, src):
            tile = keep.tile(shape, dtype, name=name, align_bytes=64)
            nc.sync.dma_start(tile[:], src)
            return tile

        rows = keep.tile([P, V], F32, name="rows")
        gate_rows = gate.rearrange("d m v -> (d m) v").rearrange("(r s) v -> r s v", r=GATE_ROWS)
        nc.sync.dma_start(rows[GATE_AT:P, :], gate_rows[:, 0, :])
        nc.sync.dma_start(rows[BIAS_AT:GATE_AT, 0:P], b.rearrange("(c p) o -> c (p o)", p=P))

        w_first = load("w_first", [P, PACK, P], F32, w_rows[:, :, 0:P])
        x_raw = [load("x_raw%d" % h, [P, PACK, HALF], F32, x_rows[:, :, h * HALF : (h + 1) * HALF]) for h in range(2)]
        lists = [load("list0", [P, V // 16], U16, lists_hbm[0])]
        w_second = load("w_second", [P, PACK, P], F32, w_rows[:, :, P : 2 * P])
        lists.extend([load("list%d" % d, [P, V // 16], U16, lists_hbm[d]) for d in range(1, 4)])
        w_rest = load("w_rest", [P, PACK, 2 * P], F32, w_rows[:, :, 2 * P : N])
        lists.extend([load("list%d" % d, [P, V // 16], U16, lists_hbm[d]) for d in range(4, D)])

        ones = keep.tile([P, P], F32, name="ones")
        nc.vector.memset(ones[:], 1.0)
        warm = keep.tile([P, 1], F32, name="warm")
        nc.scalar.activation(warm[:], ones[:, 0:1], IDENTITY, bias=ones[:, 0:1])
        quadrant = keep.tile([P, 1], F32, name="quadrant")
        nc.vector.memset(quadrant[0:32, :], 0.0)
        count = keep.tile([P, P], F32, name="count", align_bytes=64)
        nc.vector.tensor_tensor_scan(count[:], ones[:], ones[:], 0.0, MULT, ADD)
        for q in range(1, 4):
            nc.vector.memset(quadrant[32 * q : 32 * (q + 1), :], 32.0 * q)
        within = keep.tile([P, 32], F32, name="within", align_bytes=64)
        nc.vector.transpose(within[:], count[:, 0:32])
        nc.vector.memset(rows[0:BIAS_AT, :], 0.0)
        nc.vector.memset(rows[96:GATE_AT, P:V], 0.0)
        ident = keep.tile([P, P], F32, name="ident")
        nc.vector.tensor_scalar(
            ident[:], count[:], within[:, 0:1], quadrant[:], mybir.AluOpType.subtract, mybir.AluOpType.is_equal
        )

        turned = psum.tile([P, 2, P], F32, name="turned", tag="total", bufs=2)
        for h in range(2):
            nc.tensor.transpose(turned[:, h, :], rows[:, h * P : (h + 1) * P], ident[:])
        columns = keep.tile([P, 2, 16], F32, name="columns")
        nc.scalar.copy(columns[:], turned[:, :, P - 16 : P])
        bias = [columns[:, 0, 4 + blk : 5 + blk] for blk in range(BLOCKS)]
        gates = []

        def spread_gates(pair, tag):
            spread = psum.tile([P, 2, 2, P], F32, name="spread", tag=tag)
            for i in range(2):
                r = 8 - (-(2 * pair + i) * N // GATE_STEP)
                for h in range(2):
                    nc.tensor.transpose(spread[:, i, h, :], columns[:, h, r : r + 1].to_broadcast([P, P]), ident[:])
            gate_pair = keep.tile([P, 2, V], F32, name="gate_pair%d" % pair)
            nc.scalar.copy(gate_pair[:], spread[:].rearrange("p i h v -> p i (h v)"))
            gates.extend([gate_pair[:, 0, :], gate_pair[:, 1, :]])

        spread_gates(0, "sum0")
        spread_gates(1, "sum1")

        def interleave(copy, grouped, raw):
            copy(
                grouped.rearrange("p (c i) j -> p c j i", i=4),
                raw.rearrange("p j (c i) -> p c j i", i=4),
            )

        def quantise(codes, scales, grouped):
            nc.vector.quantize_mx(
                out=codes.bitcast(FP8X4), scales=scales, in_=grouped.rearrange("p c j -> p (c j)")
            )

        w_codes, w_scales = [], []

        def prepare_w(name, raw, copy, tag):
            width = raw.shape[2]
            grouped = keep.tile([P, width, PACK], BF16, name="grouped_" + name, tag=tag, align_bytes=64)
            codes = keep.tile([P, width], U32, name="codes_" + name, align_bytes=64)
            scales = keep.tile([P, width], U8, name="scales_" + name, align_bytes=64)
            interleave(copy, grouped[:], raw)
            quantise(codes[:], scales[:], grouped[:])
            for c0 in range(0, width, P):
                w_codes.append(codes[:, c0 : c0 + P])
                w_scales.append(scales[:, c0 : c0 + P])

        x_codes = keep.tile([P, T], U32, name="x_codes", align_bytes=64)
        x_scales = keep.tile([P, T], U8, name="x_scales", align_bytes=64)

        def project(blk, acc, cols):
            nc.tensor.matmul_mx(
                out=acc,
                lhsT=w_codes[blk].bitcast(FP8X4),
                lhsT_scale=w_scales[blk],
                rhs=x_codes[:, cols].bitcast(FP8X4),
                rhs_scale=x_scales[:, cols],
                start=True,
                stop=True,
            )

        y = [keep.tile([P, T], F32, name="y%d" % blk) for blk in range(BLOCKS)]

        def project_block(blk):
            acc = psum.tile([P, T], F32, name="acc", tag="acc0" if blk == 1 else "acc%d" % blk)
            project(blk, acc[:], slice(0, T))
            nc.scalar.activation(y[blk][:], acc[:], IDENTITY, bias=bias[blk])

        prepare_w("first", w_first[:], nc.vector.tensor_copy, "grouped_first")
        x_grouped = [keep.tile([P, HALF, PACK], BF16, name="x_grouped%d" % h, align_bytes=64) for h in range(2)]
        interleave(nc.vector.tensor_copy, x_grouped[0][:], x_raw[0][:])
        quantise(x_codes[:, 0:HALF], x_scales[:, 0:HALF], x_grouped[0][:])
        for c0 in (0, P):
            interleave(nc.vector.tensor_copy, x_grouped[1][:, c0 : c0 + P, :], x_raw[1][:, :, c0 : c0 + P])
        for c0 in (0, P):
            cols = slice(HALF + c0, HALF + c0 + P)
            quantise(x_codes[:, cols], x_scales[:, cols], x_grouped[1][:, c0 : c0 + P, :])
        for piece, (c0, c1) in enumerate(((0, HALF), (HALF, HALF + P), (HALF + P, T))):
            acc = psum.tile([P, c1 - c0], F32, name="acc", tag="acc%d" % piece)
            project(0, acc[:], slice(c0, c1))
            nc.scalar.activation(y[0][:, c0:c1], acc[:], IDENTITY, bias=bias[0])
        spread_gates(2, "acc1")
        prepare_w("second", w_second[:], nc.vector.tensor_copy, "grouped_second")
        project_block(1)

        for blk in range(BLOCKS):
            last = blk == BLOCKS - 1
            pe_turns = PE_TURNS_LAST if last else D
            sum_t = psum.tile([P, 2, P], F32, name="sum_t", tag="sum%d" % (blk % 2))
            for d in range(pe_turns):
                slot = "slot%d" % ((D * blk + d) % 4)
                product = keep.tile([P, V], F32, name="product%d_%d" % (blk, d), tag=slot)
                nc.vector.tensor_tensor(product[:], y[blk][:].indirect(lists[d][:]), gates[d], MULT)
                for h in range(2):
                    nc.tensor.matmul(
                        sum_t[:, h, :],
                        product[:, h * P : (h + 1) * P],
                        ident[:],
                        start=(d == 0 and h == 0),
                        stop=(d == pe_turns - 1 and h == 1),
                        is_transpose=True,
                    )
                if blk == 0 and d == 4:
                    prepare_w("third", w_rest[:, :, 0:P], nc.scalar.copy, "codes_second")
                    project_block(2)
                if blk == 0 and d == 5:
                    prepare_w("fourth", w_rest[:, :, P : 2 * P], nc.scalar.copy, "scales_second")
                    project_block(3)

            sum_t_sb = keep.tile([P, 2, P], F32, name="sum_t_sb%d" % blk)
            nc.scalar.copy(sum_t_sb[:], sum_t[:])
            total = psum.tile([P, 2, P], F32, name="total", bufs=2)
            for h in range(2):
                nc.tensor.transpose(total[:, h, :], sum_t_sb[:, h, :], ident[:])
            result = keep.tile([P, 2, P], F32, name="result%d" % blk)
            out_rows = out[blk * P : (blk + 1) * P, :]
            if not last:
                nc.scalar.copy(result[:], total[:])
                nc.sync.dma_start(out_rows, result[:].rearrange("p h v -> p (h v)"))
            else:
                fifth = keep.tile([P, V], F32, name="fifth", tag="slot2")
                nc.vector.tensor_tensor(fifth[:], y[blk][:].indirect(lists[4][:]), gates[4], MULT)
                sixth = keep.tile([P, V], F32, name="sixth", tag="slot3")
                pair = [keep.tile([P, P], F32, name="pair%d" % h) for h in range(2)]
                for h in range(2):
                    nc.vector.tensor_tensor(
                        sixth[:, h * P : (h + 1) * P], y[blk][:].indirect(lists[5][:, h * 8 : (h + 1) * 8]), gates[5][:, h * P : (h + 1) * P], MULT
                    )
                for h in range(2):
                    nc.vector.tensor_tensor(pair[h][:], fifth[:, h * P : (h + 1) * P], sixth[:, h * P : (h + 1) * P], ADD)
                for h in range(2):
                    nc.vector.tensor_tensor(result[:, h, :], total[:, h, :], pair[h][:], ADD)
                nc.sync.dma_start(out_rows, result[:].rearrange("p h v -> p (h v)"))
